import numpy as np
import ml_dtypes


def mxq(x, axis, fmt="e4m3"):
    dtype, down = {"e4m3": (ml_dtypes.float8_e4m3fn, 7), "e5m2": (ml_dtypes.float8_e5m2, 14)}[fmt]
    v = np.moveaxis(np.asarray(x, np.float32).astype(ml_dtypes.bfloat16).astype(np.float64), axis, -1)
    blocks = v.reshape(v.shape[:-1] + (-1, 32))
    amax = np.abs(blocks).max(-1, keepdims=True)
    byte = np.maximum(np.where(amax > 0, np.frexp(amax)[1] - 1 + 127, 0) - down, 1)
    scale = np.exp2(byte - 127.0)
    codes = (blocks / scale).astype(np.float32).astype(dtype).astype(np.float64)
    return np.moveaxis((codes * scale).reshape(v.shape), -1, axis)


WIDE = False


def mx_kscale(k):
    if not WIDE:
        return np.ones(k)
    levels = np.array([10, -10, 5, -5, 0])
    if k % 512:
        return np.exp2(np.random.permutation(np.resize(levels, k // 32))).repeat(32)
    a = np.empty((k // 512, 16))
    for p in range(k // 512):
        a[p, :8] = np.random.permutation(np.resize(levels, 8))
        for g in range(8):
            far = levels[np.abs(levels - a[p, g]) >= 10]
            a[p, g + 8] = far[np.random.randint(len(far))]
    return np.exp2(a.ravel()).repeat(32)


def f64(x):
    return np.asarray(x).astype(np.float64)


def striped(idx):
    return np.tile(idx.reshape(-1, 16).T, (8, 1)).astype(np.uint16)


def unstriped(offs):
    return offs[:16].T.reshape(-1).astype(np.int64)


E2M1 = np.array([0.0, 0.5, 1.0, 1.5, 2.0, 3.0, 4.0, 6.0, -0.0, -0.5, -1.0, -1.5, -2.0, -3.0, -4.0, -6.0])


def pack_weight(w, fmt):
    k, n = w.shape
    w = f64(np.asarray(w, np.float32).astype(ml_dtypes.bfloat16)).reshape(k // 32, 32, n)
    amax = np.abs(w).max(1)
    if fmt == "e4m3":
        byte = np.frexp(amax)[1] - 1 + 127 - 7
    else:
        mant, ex = np.frexp(amax / 6.0)
        byte = np.where(mant > 0.5, ex, ex - 1) + 127
    byte = np.clip(np.where(amax > 0, byte, 1), 1, 254)
    scaled = (w * np.exp2(127.0 - byte)[:, None, :]).reshape(k, n).astype(np.float32)
    by_word = np.ascontiguousarray(scaled.reshape(k // 512, 128, 4, n).transpose(0, 1, 3, 2))
    if fmt == "e4m3":
        words = by_word.astype(ml_dtypes.float8_e4m3fn).view(np.uint8)
    else:
        c = by_word.astype(ml_dtypes.float4_e2m1fn).view(np.uint8) & 0xF
        words = (c[..., 0::2] | (c[..., 1::2] << 4)).reshape(k // 512, 128, 2 * n)
    return np.ascontiguousarray(words), np.ascontiguousarray(byte.astype(np.uint8).reshape(k // 512, 16, n))


def unpack_weight(words, scales, fmt):
    g, _, n = scales.shape
    words = np.ascontiguousarray(words).reshape(g, 128, n, -1)
    if fmt == "e4m3":
        vals = words.view(ml_dtypes.float8_e4m3fn).astype(np.float64)
    else:
        nib = np.empty((g, 128, n, 4), np.uint8)
        nib[..., 0::2] = words & 0xF
        nib[..., 1::2] = words >> 4
        vals = E2M1[nib]
    vals = vals * np.repeat(np.exp2(scales.astype(np.float64) - 127.0), 8, axis=1)[..., None]
    return vals.transpose(0, 1, 3, 2).reshape(g * 512, n)


K, T, E, C, N = 1536, 512, 8, 256, 384
TOP = 4
K8 = 512


def by_expert(wq, xq):
    return np.concatenate([wq[e].T @ xq[:, e * C:(e + 1) * C] for e in range(E)], axis=1)


def setup_inputs():
    n = np.random.standard_normal
    s = mx_kscale(K)[:, None]
    deal = np.repeat(np.arange(E), C).reshape(TOP, T)[:, np.random.permutation(T)]
    deal = np.take_along_axis(deal, np.argsort(np.random.rand(TOP, T), axis=0), axis=0)
    for _ in range(8):
        s_, t_ = np.random.permutation(T).reshape(2, -1); r = np.random.randint(TOP, size=T // 2); x, y = deal[r, s_].copy(), deal[r, t_].copy()
        ok = ~((deal[:, s_] == y).any(0) | (deal[:, t_] == x).any(0)); deal[r[ok], s_[ok]] = y[ok]; deal[r[ok], t_[ok]] = x[ok]
    order = np.lexsort((np.random.rand(TOP * T), deal.reshape(-1)))
    slot_token = order % T; pos = np.empty(TOP * T, np.int64); pos[order] = np.arange(TOP * T); pos = pos.reshape(TOP, T)
    g = np.random.uniform(0.5, 1.5, (TOP, T)); g = g / g.sum(0)
    w = n((E, K, N)) / np.sqrt(K) / s[None]
    w8 = [pack_weight(m[:K8], "e4m3") for m in w]
    w4 = [pack_weight(m[K8:], "e2m1") for m in w]
    return {
        "xT": (n((K, T)) * s).astype(np.float32),
        "w8_words": np.stack([m[0] for m in w8]),
        "w8_scales": np.stack([m[1] for m in w8]),
        "w4_words": np.stack([m[0] for m in w4]),
        "w4_scales": np.stack([m[1] for m in w4]),
        "b": (0.3 * n((N, E))).astype(np.float32),
        "gate": np.stack([np.tile(r, (N, 1)) for r in g]).astype(np.float32),
        "offs": striped(slot_token),
        "pos1": striped(pos[0]),
        "pos2": striped(pos[1]),
        "pos3": striped(pos[2]),
        "pos4": striped(pos[3]),
    }


def reference(xT, w8_words, w8_scales, w4_words, w4_scales, b, gate, offs, pos1, pos2, pos3, pos4):
    idx = unstriped(offs)
    w = np.stack([np.concatenate([unpack_weight(w8_words[e], w8_scales[e], "e4m3"), unpack_weight(w4_words[e], w4_scales[e], "e2m1")]) for e in range(E)])
    xq = mxq(f64(xT)[:, idx], 0, "e4m3")
    y = by_expert(w, xq)
    y = y + np.repeat(f64(b), C, axis=1)
    return sum(f64(gate[r]) * y[:, unstriped(p)] for r, p in enumerate((pos1, pos2, pos3, pos4)))

@@ -1,0 +1,201 @@
+from contextlib import ExitStack
+
+import concourse.mybir as mybir
+
+K, T, E, C, N = 1536, 512, 8, 256, 384
+S = E * C
+FLOPS = 2 * K * N * S
+BYTES = 4 * K * T + E * K * N // 3 + E * K * N // 3 + E * K * N // 32 + 4 * N * E + 16 * T + 2 * 128 * (S + 4 * T) // 16 + 4 * N * T
+
+F32 = mybir.dt.float32
+BF16 = mybir.dt.bfloat16
+U32 = mybir.dt.uint32
+I32 = mybir.dt.int32
+U16 = mybir.dt.uint16
+U8 = mybir.dt.uint8
+FP8X4 = mybir.dt.float8_e4m3fn_x4
+FP4X4 = mybir.dt.float4_e2m1fn_x4
+COPY = mybir.ActivationFunctionType.Copy
+IDENT = mybir.ActivationFunctionType.Identity
+MULT = mybir.AluOpType.mult
+ADD = mybir.AluOpType.add
+
+P = 128
+NT = N // P
+WIN = 1376
+ROW = (4, 0, 8)
+
+
+def tile_moe_tk_lin_bias_kernel(
+    tc, xT, w8_words, w8_scales, w4_words, w4_scales, b, gate, offs, pos1, pos2, pos3, pos4, out
+):
+    nc = tc.nc
+    with ExitStack() as ctx:
+        keep = ctx.enter_context(tc.tile_pool(name="keep", bufs=1))
+        psum = ctx.enter_context(tc.psum_pool(name="psum", bufs=8))
+
+        offs_t = keep.tile([P, S // 16], U16, name="offs_t")
+        pos_t = [keep.tile([P, T // 16], U16, name="pos_t%d" % r) for r in range(4)]
+        raw = [keep.tile([P, 4, T], F32, name="raw%d" % a) for a in range(3)]
+        grp = [keep.tile([P, T, 4], BF16, name="grp%d" % a, align_bytes=64) for a in range(3)]
+        words = [keep.tile([P, WIN], U32, name="words%d" % a, align_bytes=64) for a in range(3)]
+        planes = keep.tile([P, WIN], U8, name="planes", align_bytes=64)
+        gw = [keep.tile([P, S], U32, name="gw%d" % a, align_bytes=64) for a in range(3)]
+        gp = keep.tile([P, S], U8, name="gp", align_bytes=64)
+        gp2 = keep.tile([P, S], U8, name="gp2", align_bytes=64)
+        w8 = keep.tile([P, E, 4 * N], U8, name="w8", align_bytes=64)
+        w4 = keep.tile([P, 2 * E, 2 * N], U8, name="w4", align_bytes=64)
+        s8 = keep.tile([P, E, N], U8, name="s8", align_bytes=64)
+        s4 = keep.tile([P, 2 * E, N], U8, name="s4", align_bytes=64)
+        bias = keep.tile([P, NT, E], F32, name="bias")
+        gates = keep.tile([P, 4, T], F32, name="gates")
+        y = [keep.tile([P, S], F32, name="y%d" % n) for n in range(NT)]
+
+        xv = xT.rearrange("(a p j) t -> a p j t", p=P, j=4)
+        half = T // 2
+        nc.sync.dma_start(raw[0][:, :, :half], xv[0, :, :, :half])
+        nc.sync.dma_start(raw[0][:, :, half:], xv[0, :, :, half:])
+        nc.sync.dma_start(offs_t[:], offs)
+        nc.sync.dma_start(raw[1][:], xv[1])
+        nc.sync.dma_start(raw[2][:], xv[2])
+
+        nc.gpsimd.memset(planes[:], 0)
+        nc.gpsimd.memset(gp2[:], 0)
+        nc.vector.memset(s8[:].rearrange("p e n -> p (e n)").bitcast(I32), 0)
+        nc.vector.memset(s4[:].rearrange("p e n -> p (e n)").bitcast(I32), 0)
+        for a in range(3):
+            nc.vector.memset(words[a][:, T:].bitcast(I32), 0)
+
+        v8 = w8_scales.rearrange("e a q n -> q (e a) n")
+        v4 = w4_scales.rearrange("e a q n -> q (e a) n")
+        for q in range(4):
+            nc.sync.dma_start(s8[32 * q : 32 * q + 4, :, :].bitcast(I32), v8[4 * q : 4 * q + 4].bitcast(I32))
+        for q in range(4):
+            nc.sync.dma_start(s4[32 * q : 32 * q + 4, :, :].bitcast(I32), v4[4 * q : 4 * q + 4].bitcast(I32))
+        w8v = w8_words.rearrange("e a p n r -> p (e a) (n r)")
+        w4v = w4_words.rearrange("e a p n -> p (e a) n")
+        for e in range(0, E, 2):
+            nc.sync.dma_start(w8[:, e : e + 2, :].bitcast(I32), w8v[:, e : e + 2, :].bitcast(I32))
+            nc.sync.dma_start(w4[:, 2 * e : 2 * e + 4, :].bitcast(I32), w4v[:, 2 * e : 2 * e + 4, :].bitcast(I32))
+            if e == 0:
+                nc.sync.dma_start(bias[:], b.rearrange("(c p) e -> p c e", p=P))
+        nc.sync.dma_start(gates[:], gate[:, :P, :].rearrange("r p t -> p r t"))
+        for r, pos in enumerate((pos1, pos2, pos3, pos4)):
+            nc.sync.dma_start(pos_t[r][:], pos)
+
+        def interleave(a, lo, hi, engine):
+            dst = grp[a][:, lo:hi, :].rearrange("p (c i) j -> p c j i", i=4)
+            src = raw[a][:, :, lo:hi].rearrange("p j (c i) -> p c j i", i=4)
+            if engine == 0:
+                nc.vector.tensor_copy(dst, src)
+            else:
+                nc.scalar.activation(dst, src, COPY)
+
+        def quantise(a, lo, hi):
+            nc.vector.quantize_mx(
+                out=words[a][:, lo:hi].bitcast(FP8X4),
+                scales=planes[ROW[a] :, lo:hi],
+                in_=grp[a][:, lo:hi, :].rearrange("p t j -> p (t j)"),
+            )
+
+        def gather_words(a, lo, hi):
+            nc.vector.tensor_copy(gw[a][:, lo:hi], words[a][:].indirect(offs_t[:, lo // 16 : hi // 16]))
+
+        def gather_bytes(lo, hi):
+            nc.vector.tensor_copy(gp[:, lo:hi], planes[:].indirect(offs_t[:, lo // 16 : hi // 16]))
+            for r in range(4):
+                nc.sync.dma_start(gp2[r:P:32, lo:hi].bitcast(I32), gp[8 + r : P : 32, lo:hi].bitcast(I32))
+
+        def multiply(e, n):
+            acc = psum.tile([P, C], F32, name="acc")
+            for h in range(2):
+                cols = slice(C * e + P * h, C * e + P * (h + 1))
+                for a in range(3):
+                    if a == 0:
+                        lw = w8[:, e, 4 * P * n : 4 * P * (n + 1)].bitcast(FP8X4)
+                        ls = s8[:, e, P * n : P * (n + 1)]
+                        rs = gp[ROW[0] :, cols]
+                    else:
+                        lw = w4[:, 2 * e + a - 1, 2 * P * n : 2 * P * (n + 1)].bitcast(FP4X4)
+                        ls = s4[:, 2 * e + a - 1, P * n : P * (n + 1)]
+                        rs = gp[:, cols] if a == 1 else gp2[:, cols]
+                    nc.tensor.matmul_mx(
+                        out=acc[:, P * h : P * (h + 1)],
+                        lhsT=lw,
+                        lhsT_scale=ls,
+                        rhs=gw[a][:, cols].bitcast(FP8X4),
+                        rhs_scale=rs,
+                        start=(a == 0),
+                        stop=(a == 2),
+                    )
+            nc.scalar.activation(y[n][:, C * e : C * (e + 1)], acc[:], IDENT, bias=bias[:, n, e : e + 1])
+
+        interleave(0, 0, half, 1)
+        interleave(0, half, T, 0)
+        interleave(1, 0, T, 1)
+        interleave(2, 0, T, 1)
+        quantise(0, 0, half)
+        quantise(0, half, T)
+        gather_words(0, 0, S // 2)
+        gather_words(0, S // 2, S)
+        quantise(1, 0, T)
+        gather_words(1, 0, S // 2)
+        quantise(2, 0, T)
+        gather_bytes(0, S // 2)
+        gather_bytes(S // 2, S)
+        for e in range(4):
+            gather_words(2, C * e, C * (e + 1))
+            multiply(e, 0)
+            multiply(e, 1)
+        gather_words(1, S // 2, S)
+        multiply(0, 2)
+        for e in range(4, E):
+            gather_words(2, C * e, C * (e + 1))
+            multiply(e, 0)
+        for e in range(4, E):
+            multiply(e, 1)
+        for e in range(1, E):
+            multiply(e, 2)
+
+        prod = [keep.tile([P, 4, T], F32, name="prod%d" % n) for n in range(NT)]
+        pair = [keep.tile([P, 2, T], F32, name="pair%d" % n) for n in range(NT)]
+        res = [keep.tile([P, T], F32, name="res%d" % n) for n in range(NT)]
+
+        def fetch(n, r):
+            nc.vector.tensor_tensor(prod[n][:, r, :], y[n][:].indirect(pos_t[r][:]), gates[:, r, :], MULT)
+
+        def pair_up(n):
+            nc.vector.tensor_tensor(pair[n][:], prod[n][:, 0:2, :], prod[n][:, 2:4, :], ADD)
+
+        def finish(n):
+            nc.vector.tensor_tensor(res[n][:], pair[n][:, 0, :], pair[n][:, 1, :], ADD)
+            nc.sync.dma_start(out[P * n : P * (n + 1), :], res[n][:])
+
+        for n in range(NT - 1):
+            fetch(n, 0)
+            if n:
+                pair_up(n - 1)
+            fetch(n, 1)
+            if n:
+                finish(n - 1)
+            fetch(n, 2)
+            fetch(n, 3)
+
+        n = NT - 1
+        fetch(n, 0)
+        pair_up(n - 1)
+        fetch(n, 1)
+        finish(n - 1)
+        fetch(n, 2)
+        nc.vector.tensor_tensor(pair[n][:, 0, :], prod[n][:, 0, :], prod[n][:, 1, :], ADD)
+        for h in range(2):
+            cols = slice(half * h, half * (h + 1))
+            nc.vector.tensor_tensor(
+                prod[n][:, 3, cols], y[n][:].indirect(pos_t[3][:, T // 32 * h : T // 32 * (h + 1)]), gates[:, 3, cols], MULT
+            )
+            if h == 0:
+                nc.vector.tensor_tensor(pair[n][:, 1, :], pair[n][:, 0, :], prod[n][:, 2, :], ADD)
+        for h in range(2):
+            cols = slice(half * h, half * (h + 1))
+            nc.vector.tensor_tensor(res[n][:, cols], pair[n][:, 1, cols], prod[n][:, 3, cols], ADD)
+            nc.sync.dma_start(out[P * n : P * (n + 1), cols], res[n][:, cols])

@@ -22,7 +22,7 @@ ADD = mybir.AluOpType.add
 
 P = 128
 NT = N // P
-WIN = 1376
+WIN = (1376, 704, 704)
 ROW = (4, 0, 8)
 
 
@@ -38,10 +38,11 @@ def tile_moe_tk_lin_bias_kernel(
         pos_t = [keep.tile([P, T // 16], U16, name="pos_t%d" % r) for r in range(4)]
         raw = [keep.tile([P, 4, T], F32, name="raw%d" % a) for a in range(3)]
         grp = [keep.tile([P, T, 4], BF16, name="grp%d" % a, align_bytes=64) for a in range(3)]
-        words = [keep.tile([P, WIN], U32, name="words%d" % a, align_bytes=64) for a in range(3)]
-        planes = keep.tile([P, WIN], U8, name="planes", align_bytes=64)
+        words = [keep.tile([P, WIN[a]], U32, name="words%d" % a, align_bytes=64) for a in range(3)]
+        planes = keep.tile([P, WIN[0]], U8, name="planes", align_bytes=64)
         gw = [keep.tile([P, S], U32, name="gw%d" % a, align_bytes=64) for a in range(3)]
         gp = keep.tile([P, S], U8, name="gp", align_bytes=64)
+        gp_late = keep.tile([P, S], U8, name="gp_late", align_bytes=64)
         gp2 = keep.tile([P, S], U8, name="gp2", align_bytes=64)
         w8 = keep.tile([P, E, 4 * N], U8, name="w8", align_bytes=64)
         w4 = keep.tile([P, 2 * E, 2 * N], U8, name="w4", align_bytes=64)
@@ -51,37 +52,36 @@ def tile_moe_tk_lin_bias_kernel(
         gates = keep.tile([P, 4, T], F32, name="gates")
         y = [keep.tile([P, S], F32, name="y%d" % n) for n in range(NT)]
 
+        nc.vector.memset(s8[:].rearrange("p e n -> p (e n)").bitcast(I32), 0)
         xv = xT.rearrange("(a p j) t -> a p j t", p=P, j=4)
         half = T // 2
-        nc.sync.dma_start(raw[0][:, :, :half], xv[0, :, :, :half])
-        nc.sync.dma_start(raw[0][:, :, half:], xv[0, :, :, half:])
+        cut = 256
+        nc.sync.dma_start(raw[0][:, :, :cut], xv[0, :, :, :cut])
+        nc.sync.dma_start(raw[0][:, :, cut:], xv[0, :, :, cut:])
         nc.sync.dma_start(offs_t[:], offs)
         nc.sync.dma_start(raw[1][:], xv[1])
         nc.sync.dma_start(raw[2][:], xv[2])
-
-        nc.gpsimd.memset(planes[:], 0)
-        nc.gpsimd.memset(gp2[:], 0)
-        nc.vector.memset(s8[:].rearrange("p e n -> p (e n)").bitcast(I32), 0)
-        nc.vector.memset(s4[:].rearrange("p e n -> p (e n)").bitcast(I32), 0)
-        for a in range(3):
-            nc.vector.memset(words[a][:, T:].bitcast(I32), 0)
-
         v8 = w8_scales.rearrange("e a q n -> q (e a) n")
         v4 = w4_scales.rearrange("e a q n -> q (e a) n")
         for q in range(4):
             nc.sync.dma_start(s8[32 * q : 32 * q + 4, :, :].bitcast(I32), v8[4 * q : 4 * q + 4].bitcast(I32))
-        for q in range(4):
-            nc.sync.dma_start(s4[32 * q : 32 * q + 4, :, :].bitcast(I32), v4[4 * q : 4 * q + 4].bitcast(I32))
+        nc.sync.dma_start(bias[:], b.rearrange("(c p) e -> p c e", p=P))
         w8v = w8_words.rearrange("e a p n r -> p (e a) (n r)")
         w4v = w4_words.rearrange("e a p n -> p (e a) n")
-        for e in range(0, E, 2):
-            nc.sync.dma_start(w8[:, e : e + 2, :].bitcast(I32), w8v[:, e : e + 2, :].bitcast(I32))
-            nc.sync.dma_start(w4[:, 2 * e : 2 * e + 4, :].bitcast(I32), w4v[:, 2 * e : 2 * e + 4, :].bitcast(I32))
-            if e == 0:
-                nc.sync.dma_start(bias[:], b.rearrange("(c p) e -> p c e", p=P))
-        nc.sync.dma_start(gates[:], gate[:, :P, :].rearrange("r p t -> p r t"))
+        for e in range(0, E, 4):
+            nc.sync.dma_start(w8[:, e : e + 4, :].bitcast(I32), w8v[:, e : e + 4, :].bitcast(I32))
+            nc.sync.dma_start(w4[:, 2 * e : 2 * e + 8, :].bitcast(I32), w4v[:, 2 * e : 2 * e + 8, :].bitcast(I32))
         for r, pos in enumerate((pos1, pos2, pos3, pos4)):
             nc.sync.dma_start(pos_t[r][:], pos)
+        nc.sync.dma_start(gates[:], gate[:, :P, :].rearrange("r p t -> p r t"))
+
+        nc.gpsimd.memset(s4[:].rearrange("p e n -> p (e n)").bitcast(I32), 0)
+        for q in range(4):
+            nc.gpsimd.dma_start(s4[32 * q : 32 * q + 4, :, :].bitcast(I32), v4[4 * q : 4 * q + 4].bitcast(I32))
+        nc.vector.memset(planes[:].bitcast(I32), 0)
+        for a in range(3):
+            nc.vector.memset(words[a][:, T:].bitcast(I32), 0)
+        nc.vector.memset(gp2[:].bitcast(I32), 0)
 
         def interleave(a, lo, hi, engine):
             dst = grp[a][:, lo:hi, :].rearrange("p (c i) j -> p c j i", i=4)
@@ -103,10 +103,9 @@ def tile_moe_tk_lin_bias_kernel(
 
         def gather_bytes(lo, hi):
             nc.vector.tensor_copy(gp[:, lo:hi], planes[:].indirect(offs_t[:, lo // 16 : hi // 16]))
-            for r in range(4):
-                nc.sync.dma_start(gp2[r:P:32, lo:hi].bitcast(I32), gp[8 + r : P : 32, lo:hi].bitcast(I32))
+            nc.scalar.dma_start(gp2[: P - 8, lo:hi].bitcast(I32), gp[8:, lo:hi].bitcast(I32))
 
-        def multiply(e, n):
+        def multiply(e, n, first_plane):
             acc = psum.tile([P, C], F32, name="acc")
             for h in range(2):
                 cols = slice(C * e + P * h, C * e + P * (h + 1))
@@ -114,7 +113,7 @@ def tile_moe_tk_lin_bias_kernel(
                     if a == 0:
                         lw = w8[:, e, 4 * P * n : 4 * P * (n + 1)].bitcast(FP8X4)
                         ls = s8[:, e, P * n : P * (n + 1)]
-                        rs = gp[ROW[0] :, cols]
+                        rs = first_plane[ROW[0] :, cols]
                     else:
                         lw = w4[:, 2 * e + a - 1, 2 * P * n : 2 * P * (n + 1)].bitcast(FP4X4)
                         ls = s4[:, 2 * e + a - 1, P * n : P * (n + 1)]
@@ -130,32 +129,27 @@ def tile_moe_tk_lin_bias_kernel(
                     )
             nc.scalar.activation(y[n][:, C * e : C * (e + 1)], acc[:], IDENT, bias=bias[:, n, e : e + 1])
 
-        interleave(0, 0, half, 1)
-        interleave(0, half, T, 0)
+        interleave(0, 0, cut, 1)
+        interleave(0, cut, T, 0)
         interleave(1, 0, T, 1)
         interleave(2, 0, T, 1)
-        quantise(0, 0, half)
-        quantise(0, half, T)
+        quantise(0, 0, cut)
+        quantise(0, cut, T)
         gather_words(0, 0, S // 2)
         gather_words(0, S // 2, S)
         quantise(1, 0, T)
-        gather_words(1, 0, S // 2)
         quantise(2, 0, T)
         gather_bytes(0, S // 2)
         gather_bytes(S // 2, S)
-        for e in range(4):
-            gather_words(2, C * e, C * (e + 1))
-            multiply(e, 0)
-            multiply(e, 1)
-        gather_words(1, S // 2, S)
-        multiply(0, 2)
-        for e in range(4, E):
-            gather_words(2, C * e, C * (e + 1))
-            multiply(e, 0)
-        for e in range(4, E):
-            multiply(e, 1)
-        for e in range(1, E):
-            multiply(e, 2)
+        for e in range(0, E, 2):
+            gather_words(1, C * e, C * (e + 2))
+            for f in range(e, e + 2):
+                gather_words(2, C * f, C * (f + 1))
+                multiply(f, 0, gp)
+        nc.vector.tensor_copy(gp_late[:].bitcast(I32), gp[:].bitcast(I32))
+        for n in range(1, NT):
+            for e in range(E):
+                multiply(e, n, gp if n == 1 and e < 4 else gp_late)
 
         prod = [keep.tile([P, 4, T], F32, name="prod%d" % n) for n in range(NT)]
         pair = [keep.tile([P, 2, T], F32, name="pair%d" % n) for n in range(NT)]

from contextlib import ExitStack

import concourse.mybir as mybir

K, T, E, C, N = 1536, 512, 8, 256, 384
S = E * C
FLOPS = 2 * K * N * S
BYTES = 4 * K * T + E * K * N // 3 + E * K * N // 3 + E * K * N // 32 + 4 * N * E + 16 * T + 2 * 128 * (S + 4 * T) // 16 + 4 * N * T

F32 = mybir.dt.float32
BF16 = mybir.dt.bfloat16
U32 = mybir.dt.uint32
I32 = mybir.dt.int32
U16 = mybir.dt.uint16
U8 = mybir.dt.uint8
FP8X4 = mybir.dt.float8_e4m3fn_x4
FP4X4 = mybir.dt.float4_e2m1fn_x4
COPY = mybir.ActivationFunctionType.Copy
IDENT = mybir.ActivationFunctionType.Identity
MULT = mybir.AluOpType.mult
ADD = mybir.AluOpType.add

P = 128
NT = N // P
WIN = (1376, 704, 704)
ROW = (4, 0, 8)


def tile_moe_tk_lin_bias_kernel(
    tc, xT, w8_words, w8_scales, w4_words, w4_scales, b, gate, offs, pos1, pos2, pos3, pos4, out
):
    nc = tc.nc
    with ExitStack() as ctx:
        keep = ctx.enter_context(tc.tile_pool(name="keep", bufs=1))
        psum = ctx.enter_context(tc.psum_pool(name="psum", bufs=8))

        offs_t = keep.tile([P, S // 16], U16, name="offs_t")
        pos_t = [keep.tile([P, T // 16], U16, name="pos_t%d" % r) for r in range(4)]
        raw = [keep.tile([P, 4, T], F32, name="raw%d" % a) for a in range(3)]
        grp = [keep.tile([P, T, 4], BF16, name="grp%d" % a, align_bytes=64) for a in range(3)]
        words = [keep.tile([P, WIN[a]], U32, name="words%d" % a, align_bytes=64) for a in range(3)]
        planes = keep.tile([P, WIN[0]], U8, name="planes", align_bytes=64)
        gw = [keep.tile([P, S], U32, name="gw%d" % a, align_bytes=64) for a in range(3)]
        gp = keep.tile([P, S], U8, name="gp", align_bytes=64)
        gp_late = keep.tile([P, S], U8, name="gp_late", align_bytes=64)
        gp2 = keep.tile([P, S], U8, name="gp2", align_bytes=64)
        w8 = keep.tile([P, E, 4 * N], U8, name="w8", align_bytes=64)
        w4 = keep.tile([P, 2 * E, 2 * N], U8, name="w4", align_bytes=64)
        s8 = keep.tile([P, E, N], U8, name="s8", align_bytes=64)
        s4 = keep.tile([P, 2 * E, N], U8, name="s4", align_bytes=64)
        bias = keep.tile([P, NT, E], F32, name="bias")
        gates = keep.tile([P, 4, T], F32, name="gates")
        y = [keep.tile([P, S], F32, name="y%d" % n) for n in range(NT)]

        nc.vector.memset(s8[:].rearrange("p e n -> p (e n)").bitcast(I32), 0)
        xv = xT.rearrange("(a p j) t -> a p j t", p=P, j=4)
        half = T // 2
        cut = 256
        nc.sync.dma_start(raw[0][:, :, :cut], xv[0, :, :, :cut])
        nc.sync.dma_start(raw[0][:, :, cut:], xv[0, :, :, cut:])
        nc.sync.dma_start(offs_t[:], offs)
        nc.sync.dma_start(raw[1][:], xv[1])
        nc.sync.dma_start(raw[2][:], xv[2])
        v8 = w8_scales.rearrange("e a q n -> q (e a) n")
        v4 = w4_scales.rearrange("e a q n -> q (e a) n")
        for q in range(4):
            nc.sync.dma_start(s8[32 * q : 32 * q + 4, :, :].bitcast(I32), v8[4 * q : 4 * q + 4].bitcast(I32))
        nc.sync.dma_start(bias[:], b.rearrange("(c p) e -> p c e", p=P))
        w8v = w8_words.rearrange("e a p n r -> p (e a) (n r)")
        w4v = w4_words.rearrange("e a p n -> p (e a) n")
        for e in range(0, E, 4):
            nc.sync.dma_start(w8[:, e : e + 4, :].bitcast(I32), w8v[:, e : e + 4, :].bitcast(I32))
            nc.sync.dma_start(w4[:, 2 * e : 2 * e + 8, :].bitcast(I32), w4v[:, 2 * e : 2 * e + 8, :].bitcast(I32))
        for r, pos in enumerate((pos1, pos2, pos3, pos4)):
            nc.sync.dma_start(pos_t[r][:], pos)
        nc.sync.dma_start(gates[:], gate[:, :P, :].rearrange("r p t -> p r t"))

        nc.gpsimd.memset(s4[:].rearrange("p e n -> p (e n)").bitcast(I32), 0)
        for q in range(4):
            nc.gpsimd.dma_start(s4[32 * q : 32 * q + 4, :, :].bitcast(I32), v4[4 * q : 4 * q + 4].bitcast(I32))
        nc.vector.memset(planes[:].bitcast(I32), 0)
        for a in range(3):
            nc.vector.memset(words[a][:, T:].bitcast(I32), 0)
        nc.vector.memset(gp2[:].bitcast(I32), 0)

        def interleave(a, lo, hi, engine):
            dst = grp[a][:, lo:hi, :].rearrange("p (c i) j -> p c j i", i=4)
            src = raw[a][:, :, lo:hi].rearrange("p j (c i) -> p c j i", i=4)
            if engine == 0:
                nc.vector.tensor_copy(dst, src)
            else:
                nc.scalar.activation(dst, src, COPY)

        def quantise(a, lo, hi):
            nc.vector.quantize_mx(
                out=words[a][:, lo:hi].bitcast(FP8X4),
                scales=planes[ROW[a] :, lo:hi],
                in_=grp[a][:, lo:hi, :].rearrange("p t j -> p (t j)"),
            )

        def gather_words(a, lo, hi):
            nc.vector.tensor_copy(gw[a][:, lo:hi], words[a][:].indirect(offs_t[:, lo // 16 : hi // 16]))

        def gather_bytes(lo, hi):
            nc.vector.tensor_copy(gp[:, lo:hi], planes[:].indirect(offs_t[:, lo // 16 : hi // 16]))
            nc.scalar.dma_start(gp2[: P - 8, lo:hi].bitcast(I32), gp[8:, lo:hi].bitcast(I32))

        def multiply(e, n, first_plane):
            acc = psum.tile([P, C], F32, name="acc")
            for h in range(2):
                cols = slice(C * e + P * h, C * e + P * (h + 1))
                for a in range(3):
                    if a == 0:
                        lw = w8[:, e, 4 * P * n : 4 * P * (n + 1)].bitcast(FP8X4)
                        ls = s8[:, e, P * n : P * (n + 1)]
                        rs = first_plane[ROW[0] :, cols]
                    else:
                        lw = w4[:, 2 * e + a - 1, 2 * P * n : 2 * P * (n + 1)].bitcast(FP4X4)
                        ls = s4[:, 2 * e + a - 1, P * n : P * (n + 1)]
                        rs = gp[:, cols] if a == 1 else gp2[:, cols]
                    nc.tensor.matmul_mx(
                        out=acc[:, P * h : P * (h + 1)],
                        lhsT=lw,
                        lhsT_scale=ls,
                        rhs=gw[a][:, cols].bitcast(FP8X4),
                        rhs_scale=rs,
                        start=(a == 0),
                        stop=(a == 2),
                    )
            nc.scalar.activation(y[n][:, C * e : C * (e + 1)], acc[:], IDENT, bias=bias[:, n, e : e + 1])

        interleave(0, 0, cut, 1)
        interleave(0, cut, T, 0)
        interleave(1, 0, T, 1)
        interleave(2, 0, T, 1)
        quantise(0, 0, cut)
        quantise(0, cut, T)
        gather_words(0, 0, S // 2)
        gather_words(0, S // 2, S)
        quantise(1, 0, T)
        quantise(2, 0, T)
        gather_bytes(0, S // 2)
        gather_bytes(S // 2, S)
        for e in range(0, E, 2):
            gather_words(1, C * e, C * (e + 2))
            for f in range(e, e + 2):
                gather_words(2, C * f, C * (f + 1))
                multiply(f, 0, gp)
        nc.vector.tensor_copy(gp_late[:].bitcast(I32), gp[:].bitcast(I32))
        for n in range(1, NT):
            for e in range(E):
                multiply(e, n, gp if n == 1 and e < 4 else gp_late)

        prod = [keep.tile([P, 4, T], F32, name="prod%d" % n) for n in range(NT)]
        pair = [keep.tile([P, 2, T], F32, name="pair%d" % n) for n in range(NT)]
        res = [keep.tile([P, T], F32, name="res%d" % n) for n in range(NT)]

        def fetch(n, r):
            nc.vector.tensor_tensor(prod[n][:, r, :], y[n][:].indirect(pos_t[r][:]), gates[:, r, :], MULT)

        def pair_up(n):
            nc.vector.tensor_tensor(pair[n][:], prod[n][:, 0:2, :], prod[n][:, 2:4, :], ADD)

        def finish(n):
            nc.vector.tensor_tensor(res[n][:], pair[n][:, 0, :], pair[n][:, 1, :], ADD)
            nc.sync.dma_start(out[P * n : P * (n + 1), :], res[n][:])

        for n in range(NT - 1):
            fetch(n, 0)
            if n:
                pair_up(n - 1)
            fetch(n, 1)
            if n:
                finish(n - 1)
            fetch(n, 2)
            fetch(n, 3)

        n = NT - 1
        fetch(n, 0)
        pair_up(n - 1)
        fetch(n, 1)
        finish(n - 1)
        fetch(n, 2)
        nc.vector.tensor_tensor(pair[n][:, 0, :], prod[n][:, 0, :], prod[n][:, 1, :], ADD)
        for h in range(2):
            cols = slice(half * h, half * (h + 1))
            nc.vector.tensor_tensor(
                prod[n][:, 3, cols], y[n][:].indirect(pos_t[3][:, T // 32 * h : T // 32 * (h + 1)]), gates[:, 3, cols], MULT
            )
            if h == 0:
                nc.vector.tensor_tensor(pair[n][:, 1, :], pair[n][:, 0, :], prod[n][:, 2, :], ADD)
        for h in range(2):
            cols = slice(half * h, half * (h + 1))
            nc.vector.tensor_tensor(res[n][:, cols], pair[n][:, 1, cols], prod[n][:, 3, cols], ADD)
            nc.sync.dma_start(out[P * n : P * (n + 1), cols], res[n][:, cols])
